import numpy as np
import ml_dtypes


def mxq(x, axis, fmt="e4m3"):
    dtype, down = {"e4m3": (ml_dtypes.float8_e4m3fn, 7), "e5m2": (ml_dtypes.float8_e5m2, 14)}[fmt]
    v = np.moveaxis(np.asarray(x, np.float32).astype(ml_dtypes.bfloat16).astype(np.float64), axis, -1)
    blocks = v.reshape(v.shape[:-1] + (-1, 32))
    amax = np.abs(blocks).max(-1, keepdims=True)
    byte = np.maximum(np.where(amax > 0, np.frexp(amax)[1] - 1 + 127, 0) - down, 1)
    scale = np.exp2(byte - 127.0)
    codes = (blocks / scale).astype(np.float32).astype(dtype).astype(np.float64)
    return np.moveaxis((codes * scale).reshape(v.shape), -1, axis)


WIDE = False


def mx_kscale(k):
    if not WIDE:
        return np.ones(k)
    levels = np.array([10, -10, 5, -5, 0])
    if k % 512:
        return np.exp2(np.random.permutation(np.resize(levels, k // 32))).repeat(32)
    a = np.empty((k // 512, 16))
    for p in range(k // 512):
        a[p, :8] = np.random.permutation(np.resize(levels, 8))
        for g in range(8):
            far = levels[np.abs(levels - a[p, g]) >= 10]
            a[p, g + 8] = far[np.random.randint(len(far))]
    return np.exp2(a.ravel()).repeat(32)


def f64(x):
    return np.asarray(x).astype(np.float64)


def striped(idx):
    return np.tile(idx.reshape(-1, 16).T, (8, 1)).astype(np.uint16)


def unstriped(offs):
    return offs[:16].T.reshape(-1).astype(np.int64)


def striped8(idx):
    return np.concatenate([x.reshape(-1, 16).T for x in idx]).astype(np.uint16)


def runs(offs, k):
    lists = np.stack([offs[16 * r : 16 * r + 16].T.reshape(-1) for r in range(8)]).astype(np.int64)
    return lists[np.arange(k) % 512 // 64]


def pack_weight(w):
    k, n = w.shape
    w = f64(np.asarray(w, np.float32).astype(ml_dtypes.bfloat16)).reshape(k // 32, 32, n)
    amax = np.abs(w).max(1)
    byte = np.clip(np.where(amax > 0, np.frexp(amax)[1] - 1 + 127 - 7, 1), 1, 254)
    scaled = (w * np.exp2(127.0 - byte)[:, None, :]).reshape(k, n).astype(np.float32)
    words = np.ascontiguousarray(scaled.reshape(k // 512, 128, 4, n).transpose(0, 1, 3, 2)).astype(ml_dtypes.float8_e4m3fn).view(np.uint8)
    return words, np.ascontiguousarray(byte.astype(np.uint8).reshape(k // 512, 16, n))


def unpack_weight(words, scales):
    g, p, n, _ = words.shape
    vals = np.ascontiguousarray(words).view(ml_dtypes.float8_e4m3fn).astype(np.float64) * np.repeat(np.exp2(scales.astype(np.float64) - 127.0), 8, axis=1)[..., None]
    return vals.transpose(0, 1, 3, 2).reshape(g * 512, n)


def sigmoid(v):
    return 1.0 / (1.0 + np.exp(-np.maximum(v, -700.0)))


K, T, S, N, G, H = 512, 2048, 512, 512, 2048, 512


def setup_inputs():
    n = np.random.standard_normal
    s = mx_kscale(K)[:, None]
    u = mx_kscale(S)
    packed_xT = pack_weight(n((K, T)) * s)
    packed_dT = pack_weight(n((K, G)) / s)
    return {
        "x_words": packed_xT[0],
        "x_scales": packed_xT[1],
        "d_words": packed_dT[0],
        "d_scales": packed_dT[1],
        "gn": (np.random.uniform(0.5, 1.5, (H, 1)) * u[:, None]).astype(np.float32),
        "w1": (n((H, N)) / np.sqrt(H) / u[:, None]).astype(np.float32),
        "offs": striped8(np.random.randint(0, T, (8, S))),
        "k1": striped8(np.random.randint(0, G, (8, H))),
        "n1": striped(np.random.permutation(S)),
        "n2": striped(np.random.permutation(S)),
        "n3": striped(np.random.permutation(S)),
        "n4": striped(np.random.permutation(S)),
    }


def reference(x_words, x_scales, d_words, d_scales, gn, w1, offs, k1, n1, n2, n3, n4):
    d_k1 = unpack_weight(d_words, d_scales)[np.arange(K)[:, None], runs(k1, K)]
    xq = unpack_weight(x_words, x_scales)[np.arange(K)[:, None], runs(offs, K)]
    h = 0.0625 * (d_k1.T @ xq)
    z = f64(gn) * (h + (sigmoid(h[:, unstriped(n1)])) * (h[:, unstriped(n2)] - h))
    h2 = mxq(f64(w1), 0, "e4m3").T @ mxq(z, 0, "e4m3")
    return 0.75 * (h2[:, unstriped(n3)] + h2[:, unstriped(n4)]) - h2

@@ -1,0 +1,295 @@
+from contextlib import ExitStack
+
+import concourse.mybir as mybir
+
+F32 = mybir.dt.float32
+BF16 = mybir.dt.bfloat16
+I32 = mybir.dt.int32
+U32 = mybir.dt.uint32
+U16 = mybir.dt.uint16
+U8 = mybir.dt.uint8
+FP8X4 = mybir.dt.float8_e4m3fn_x4
+ALU = mybir.AluOpType
+ACT = mybir.ActivationFunctionType
+
+P = 128
+PACK = 4
+T = 2048
+S = 512
+HALF = 256
+FLOPS = 2 * 2 * 512 * 512 * 512
+BIG = 3.0e38
+
+
+def tile_picked_hpqtracklap_none_p_kernel(tc, x_words, x_scales, d_words, d_scales, gn, w1, offs, k1, n1, n2, n3, n4, out):
+    nc = tc.nc
+    with ExitStack() as ctx:
+        keep = ctx.enter_context(tc.tile_pool(name="keep", bufs=1))
+        psum = ctx.enter_context(tc.psum_pool(name="psum", bufs=1))
+
+        def entries(lst, half):
+            return lst[:, half * HALF // 16 : (half + 1) * HALF // 16]
+
+        def cols(half):
+            return slice(half * HALF, (half + 1) * HALF)
+
+        d_rows = keep.tile([P, T], U8, name="d_rows")
+        x_rows = keep.tile([P, T], U8, name="x_rows")
+        planes = keep.tile([P, 2 * S], U8, name="planes", align_bytes=64)
+        nc.vector.memset(x_rows[:].bitcast(I32), 0)
+        nc.gpsimd.memset(d_rows[:, 0 : T // 2].bitcast(I32), 0)
+        nc.vector.memset(d_rows[:, T // 2 : T].bitcast(I32), 0)
+        nc.vector.memset(planes[:].bitcast(I32), 0)
+
+        lists = {}
+        for name in ("offs", "k1", "n1", "n2", "n3", "n4"):
+            lists[name] = keep.tile([P, S // 16], U16, name="list_" + name)
+        gain = keep.tile([P, PACK], F32, name="gain")
+        d_table = keep.tile([P, T], U32, name="d_table")
+        x_table = keep.tile([P, T], U32, name="x_table")
+
+        nc.sync.dma_start(lists["offs"][:], offs)
+        nc.sync.dma_start(lists["k1"][:], k1)
+        nc.sync.dma_start(x_rows[0:P:8, :].bitcast(I32), x_scales[0].bitcast(I32))
+        nc.sync.dma_start(d_rows[0:P:8, :].bitcast(I32), d_scales[0].bitcast(I32))
+        nc.sync.dma_start(gain[:], gn.rearrange("(p t) o -> p (t o)", t=PACK))
+        nc.sync.dma_start(lists["n1"][:], n1)
+        nc.sync.dma_start(lists["n2"][:], n2)
+        nc.sync.dma_start(d_table[:].bitcast(I32), d_words[0].rearrange("p n t -> p (n t)").bitcast(I32))
+        nc.sync.dma_start(x_table[:].bitcast(I32), x_words[0].rearrange("p n t -> p (n t)").bitcast(I32))
+        nc.sync.dma_start(lists["n3"][:], n3)
+        nc.sync.dma_start(lists["n4"][:], n4)
+
+        x_bytes = keep.tile([P, S], U8, name="x_bytes")
+        d_bytes = keep.tile([P, S], U8, name="d_bytes", tag="d_gathered")
+        staged = keep.tile([P, 2 * S], U8, name="staged", tag="early")
+        nc.vector.tensor_copy(x_bytes[:], x_rows[:].indirect(lists["offs"][:]))
+        nc.vector.tensor_copy(d_bytes[:], d_rows[:].indirect(lists["k1"][:]))
+        nc.vector.tensor_copy(staged[:, S : 2 * S].bitcast(I32), x_bytes[:].bitcast(I32))
+        nc.vector.tensor_copy(
+            staged[:, 0:S].rearrange("p (t m) -> p t m", t=PACK),
+            d_bytes[:].rearrange("p (m t) -> p t m", t=PACK),
+        )
+        for q in range(4):
+            nc.scalar.dma_start(
+                planes[32 * q : 32 * q + 4, :].bitcast(I32),
+                staged[32 * q : 32 * q + 32 : 8, :].bitcast(I32),
+            )
+
+        w_raw = keep.tile([P, PACK, S], F32, name="w_raw", tag="early")
+        nc.sync.dma_start(w_raw[:], w1.rearrange("(p t) m -> p t m", t=PACK))
+        gain16 = keep.tile([P, PACK], F32, name="gain16")
+        inv_raw = keep.tile([P, PACK], F32, name="inv_raw")
+        inv_gain = keep.tile([P, PACK], F32, name="inv_gain")
+        d_picked = keep.tile([P, S], U32, name="d_picked", tag="d_gathered")
+        d_codes = keep.tile([P, S], U32, name="d_codes", align_bytes=64)
+        x_codes = keep.tile([P, S], U32, name="x_codes", align_bytes=64)
+        nc.vector.tensor_copy(d_picked[:], d_table[:].indirect(lists["k1"][:]))
+        nc.vector.reciprocal(inv_raw[:], gain[:])
+        nc.vector.tensor_copy(
+            d_codes[:].rearrange("p (t m i) -> p m t i", t=PACK, i=PACK),
+            d_picked[:].rearrange("p (m i t) -> p m t i", t=PACK, i=PACK),
+        )
+        nc.gpsimd.tensor_scalar(gain16[:], gain[:], 0.0625, 0.0, ALU.mult, ALU.add)
+        nc.gpsimd.tensor_scalar(inv_gain[:], inv_raw[:], BIG, -BIG, ALU.min, ALU.max)
+        nc.vector.tensor_copy(x_codes[:], x_table[:].indirect(lists["offs"][:]))
+
+        gh = [keep.tile([P, S], F32, name="gh%d" % t) for t in range(PACK)]
+        gate = [keep.tile([P, PACK, HALF], F32, name="gate%d" % half) for half in range(2)]
+        far = [keep.tile([P, PACK, HALF], F32, name="far%d" % half) for half in range(2)]
+        near = [keep.tile([P, PACK, HALF], F32, name="near%d" % half) for half in range(2)]
+        fetched = keep.tile([P, PACK, HALF], F32, name="fetched")
+        def first_product(t, bank, a, n):
+            nc.tensor.matmul_mx(
+                out=bank[:],
+                lhsT=d_codes[:, t * P : (t + 1) * P].bitcast(FP8X4),
+                lhsT_scale=planes[:, t * P : (t + 1) * P],
+                rhs=x_codes[:, a : a + n].bitcast(FP8X4),
+                rhs_scale=planes[:, S + a : S + a + n],
+                start=True,
+                stop=True,
+            )
+
+        def empty_h(t):
+            if t < 2:
+                for half in range(2):
+                    bank = psum.tile([P, HALF], F32, name="h%d%d" % (t, half), tag="bank%d" % (2 * t + half))
+                    first_product(t, bank, half * HALF, HALF)
+                    nc.vector.tensor_scalar(gh[t][:, cols(half)], bank[:], gain16[:, t : t + 1], None, ALU.mult)
+            else:
+                bank = psum.tile([P, S], F32, name="h%d" % t, tag="bank%d" % (2 * (t - 2) + 1))
+                first_product(t, bank, 0, S)
+                nc.scalar.activation(gh[t][:], bank[:], ACT.Copy, scale=gain16[:, t : t + 1])
+
+        shared = [(2, 1), (3, 1)]
+
+        def gate_of(t, half):
+            nc.scalar.activation(gate[half][:, t, :], gh[t][:].indirect(entries(lists["n1"], half)), ACT.Sigmoid, scale=inv_gain[:, t : t + 1])
+
+        def fetch(t, half):
+            nc.scalar.activation(fetched[:, t, :], gh[t][:].indirect(entries(lists["n2"], half)), ACT.Copy)
+
+        def blend(t, half):
+            if (t, half) in shared:
+                nc.vector.tensor_tensor(far[half][:, t, :], fetched[:, t, :], gate[half][:, t, :], ALU.mult)
+            else:
+                nc.vector.tensor_tensor(far[half][:, t, :], gh[t][:].indirect(entries(lists["n2"], half)), gate[half][:, t, :], ALU.mult)
+            nc.vector.scalar_tensor_tensor(near[half][:, t, :], gate[half][:, t, :], 1.0, gh[t][:, cols(half)], ALU.subtract, ALU.mult)
+
+        pieces = [(0, 256), (256, 128), (384, 128)]
+        z_bf = [keep.tile([P, PACK * n], BF16, name="z_bf%d" % k, align_bytes=64) for k, (a, n) in enumerate(pieces)]
+        z_codes = [keep.tile([P, n], U32, name="z_codes%d" % k, align_bytes=64) for k, (a, n) in enumerate(pieces)]
+        z_scales = [keep.tile([P, n], U8, name="z_scales%d" % k, align_bytes=64) for k, (a, n) in enumerate(pieces)]
+
+        def round_z(k):
+            a, n = pieces[k]
+            half = a // HALF
+            within = slice(a % HALF, a % HALF + n)
+            nc.vector.tensor_tensor(
+                z_bf[k][:].rearrange("p (c i t) -> p c t i", i=2, t=PACK),
+                far[half][:, :, within].rearrange("p t (c i) -> p c t i", i=2),
+                near[half][:, :, within].rearrange("p t (c i) -> p c t i", i=2),
+                ALU.subtract,
+            )
+
+        def quantize_z(k):
+            nc.vector.quantize_mx(out=z_codes[k][:].bitcast(FP8X4), scales=z_scales[k][:], in_=z_bf[k][:])
+
+        w_bf = [keep.tile([P, PACK * HALF], BF16, name="w_bf%d" % half, align_bytes=64) for half in range(2)]
+        w_codes = [keep.tile([P, HALF], U32, name="w_codes%d" % half, align_bytes=64) for half in range(2)]
+        w_scales = [keep.tile([P, HALF], U8, name="w_scales%d" % half, align_bytes=64) for half in range(2)]
+
+        def round_w(half):
+            nc.scalar.copy(
+                w_bf[half][:].rearrange("p (c i t) -> p c t i", i=4, t=PACK),
+                w_raw[:, :, cols(half)].rearrange("p t (c i) -> p c t i", i=4),
+            )
+
+        def quantize_w(half):
+            nc.vector.quantize_mx(out=w_codes[half][:].bitcast(FP8X4), scales=w_scales[half][:], in_=w_bf[half][:])
+
+        banks2 = {}
+        scaled = [keep.tile([P, S], F32, name="scaled%d" % b) for b in range(PACK)]
+        third = [keep.tile([P, S], F32, name="third%d" % b) for b in range(PACK)]
+        both = [keep.tile([P, S], F32, name="both%d" % b) for b in range(PACK)]
+        result = [keep.tile([P, S], F32, name="result%d" % b) for b in range(PACK)]
+        fourth = keep.tile([P, S], F32, name="fourth")
+        negated = keep.tile([P, HALF], F32, name="negated")
+        for b in range(PACK):
+            for half in range(2):
+                banks2[b, half] = psum.tile([P, HALF], F32, name="h2_%d%d" % (b, half), tag="bank%d" % (2 * b + half))
+
+        def second_product(k, b):
+            a, n = pieces[k]
+            within = slice((b % 2) * P, (b % 2 + 1) * P)
+            nc.tensor.matmul_mx(
+                out=banks2[b, a // HALF][:, a % HALF : a % HALF + n],
+                lhsT=w_codes[b // 2][:, within].bitcast(FP8X4),
+                lhsT_scale=w_scales[b // 2][:, within],
+                rhs=z_codes[k][:].bitcast(FP8X4),
+                rhs_scale=z_scales[k][:],
+                start=True,
+                stop=True,
+            )
+
+        def empty_h2(b, half, engine):
+            if engine == "scalar":
+                nc.scalar.activation(scaled[b][:, cols(half)], banks2[b, half][:], ACT.Copy, scale=0.75)
+            else:
+                nc.vector.tensor_scalar(scaled[b][:, cols(half)], banks2[b, half][:], 0.75, None, ALU.mult)
+
+        def fetch3(b, half):
+            nc.scalar.activation(third[b][:, cols(half)], scaled[b][:].indirect(entries(lists["n3"], half)), ACT.Copy)
+
+        def fetch4(b, half):
+            nc.scalar.activation(fourth[:, cols(half)], scaled[b][:].indirect(entries(lists["n4"], half)), ACT.Copy)
+
+        def add4(b, half):
+            nc.vector.tensor_tensor(both[b][:, cols(half)], scaled[b][:].indirect(entries(lists["n4"], half)), third[b][:, cols(half)], ALU.add)
+
+        def add_plain(b, half):
+            nc.vector.tensor_tensor(both[b][:, cols(half)], fourth[:, cols(half)], third[b][:, cols(half)], ALU.add)
+
+        def less_h2(b, half):
+            nc.vector.tensor_tensor(result[b][:, cols(half)], both[b][:, cols(half)], banks2[b, half][:], ALU.subtract)
+
+        def store(b, half):
+            if half is None:
+                nc.sync.dma_start(out[b * P : (b + 1) * P, :], result[b][:])
+            else:
+                nc.sync.dma_start(out[b * P : (b + 1) * P, cols(half)], result[b][:, cols(half)])
+
+        empty_h(0)
+        gate_of(0, 0)
+        empty_h(1)
+        gate_of(1, 0)
+        gate_of(0, 1)
+        gate_of(1, 1)
+        empty_h(2)
+        gate_of(2, 0)
+        empty_h(3)
+        gate_of(3, 0)
+        gate_of(2, 1)
+        gate_of(3, 1)
+        for t, half in shared:
+            fetch(t, half)
+        round_w(0)
+        round_w(1)
+        blend(0, 0)
+        blend(1, 0)
+        blend(0, 1)
+        blend(1, 1)
+        blend(2, 0)
+        blend(3, 0)
+        round_z(0)
+        blend(2, 1)
+        quantize_z(0)
+        quantize_w(0)
+        blend(3, 1)
+        quantize_w(1)
+        round_z(1)
+        round_z(2)
+        quantize_z(1)
+        quantize_z(2)
+        for b in range(PACK):
+            second_product(0, b)
+        for b in range(PACK):
+            empty_h2(b, 0, "scalar")
+        nc.scalar.activation(negated[:], banks2[0, 0][:], ACT.Copy, scale=-1.0)
+        for b in range(PACK):
+            second_product(1, b)
+            second_product(2, b)
+        empty_h2(0, 1, "vector")
+        nc.vector.tensor_tensor(both[0][:, cols(0)], scaled[0][:].indirect(entries(lists["n4"], 0)), negated[:], ALU.add)
+        empty_h2(1, 1, "scalar")
+        fetch3(0, 1)
+        nc.vector.tensor_tensor(result[0][:, cols(0)], scaled[0][:].indirect(entries(lists["n3"], 0)), both[0][:, cols(0)], ALU.add)
+        add4(0, 1)
+        fetch3(1, 0)
+        fetch3(1, 1)
+        add4(1, 0)
+        less_h2(0, 1)
+        store(0, None)
+        empty_h2(2, 1, "scalar")
+        fetch3(2, 0)
+        fetch3(2, 1)
+        add4(1, 1)
+        less_h2(1, 0)
+        add4(2, 0)
+        less_h2(1, 1)
+        store(1, None)
+        empty_h2(3, 1, "scalar")
+        fetch3(3, 0)
+        fetch4(3, 0)
+        fetch3(3, 1)
+        fetch4(3, 1)
+        add4(2, 1)
+        less_h2(2, 0)
+        less_h2(2, 1)
+        store(2, None)
+        add_plain(3, 0)
+        less_h2(3, 0)
+        store(3, 0)
+        add_plain(3, 1)
+        less_h2(3, 1)
+        store(3, 1)

@@ -41,6 +41,11 @@ def tile_picked_hpqtracklap_none_p_kernel(tc, x_words, x_scales, d_words, d_scal
         nc.vector.memset(d_rows[:, T // 2 : T].bitcast(I32), 0)
         nc.vector.memset(planes[:].bitcast(I32), 0)
 
+        warm_in = keep.tile([P, 1], F32, name="warm_in")
+        warm_out = keep.tile([P, 1], F32, name="warm_out")
+        nc.vector.memset(warm_in[:], 0.0)
+        nc.scalar.activation(warm_out[:], warm_in[:], ACT.Sigmoid)
+
         lists = {}
         for name in ("offs", "k1", "n1", "n2", "n3", "n4"):
             lists[name] = keep.tile([P, S // 16], U16, name="list_" + name)

@@ -17,6 +17,7 @@ PACK = 4
 T = 2048
 S = 512
 HALF = 256
+SPARE = 16
 FLOPS = 2 * 2 * 512 * 512 * 512
 BIG = 3.0e38
 
@@ -27,31 +28,29 @@ def tile_picked_hpqtracklap_none_p_kernel(tc, x_words, x_scales, d_words, d_scal
         keep = ctx.enter_context(tc.tile_pool(name="keep", bufs=1))
         psum = ctx.enter_context(tc.psum_pool(name="psum", bufs=1))
 
-        def entries(lst, half):
-            return lst[:, half * HALF // 16 : (half + 1) * HALF // 16]
+        def entries(name, a, n):
+            return lists[name][:, a // 16 : (a + n) // 16]
 
-        def cols(half):
-            return slice(half * HALF, (half + 1) * HALF)
-
-        d_rows = keep.tile([P, T], U8, name="d_rows")
         x_rows = keep.tile([P, T], U8, name="x_rows")
-        planes = keep.tile([P, 2 * S], U8, name="planes", align_bytes=64)
+        d_rows = keep.tile([P, T], U8, name="d_rows")
+        moved = keep.tile([P, 2 * S], U8, name="moved", align_bytes=64)
+        scaled = [keep.tile([P, S + SPARE], F32, name="scaled%d" % b) for b in range(PACK)]
         nc.vector.memset(x_rows[:].bitcast(I32), 0)
-        nc.gpsimd.memset(d_rows[:, 0 : T // 2].bitcast(I32), 0)
-        nc.vector.memset(d_rows[:, T // 2 : T].bitcast(I32), 0)
-        nc.vector.memset(planes[:].bitcast(I32), 0)
-
+        nc.vector.memset(d_rows[:].bitcast(I32), 0)
         warm_in = keep.tile([P, 1], F32, name="warm_in")
         warm_out = keep.tile([P, 1], F32, name="warm_out")
         nc.vector.memset(warm_in[:], 0.0)
         nc.scalar.activation(warm_out[:], warm_in[:], ACT.Sigmoid)
+        nc.vector.memset(moved[:].bitcast(I32), 0)
+        for b in range(PACK):
+            nc.vector.memset(scaled[b][:, S : S + SPARE], 0.0)
 
         lists = {}
         for name in ("offs", "k1", "n1", "n2", "n3", "n4"):
             lists[name] = keep.tile([P, S // 16], U16, name="list_" + name)
         gain = keep.tile([P, PACK], F32, name="gain")
-        d_table = keep.tile([P, T], U32, name="d_table")
-        x_table = keep.tile([P, T], U32, name="x_table")
+        d_table = keep.tile([P, T], U32, name="d_table", tag="d_table")
+        x_table = keep.tile([P, T], U32, name="x_table", tag="x_table")
 
         nc.sync.dma_start(lists["offs"][:], offs)
         nc.sync.dma_start(lists["k1"][:], k1)
@@ -66,80 +65,78 @@ def tile_picked_hpqtracklap_none_p_kernel(tc, x_words, x_scales, d_words, d_scal
         nc.sync.dma_start(lists["n4"][:], n4)
 
         x_bytes = keep.tile([P, S], U8, name="x_bytes")
-        d_bytes = keep.tile([P, S], U8, name="d_bytes", tag="d_gathered")
-        staged = keep.tile([P, 2 * S], U8, name="staged", tag="early")
+        d_bytes = keep.tile([P, S], U8, name="d_bytes", tag="d_bytes")
+        staged = keep.tile([P, 2 * S], U8, name="staged", tag="staged")
         nc.vector.tensor_copy(x_bytes[:], x_rows[:].indirect(lists["offs"][:]))
         nc.vector.tensor_copy(d_bytes[:], d_rows[:].indirect(lists["k1"][:]))
-        nc.vector.tensor_copy(staged[:, S : 2 * S].bitcast(I32), x_bytes[:].bitcast(I32))
+        nc.vector.tensor_copy(staged[:, 0:S].bitcast(I32), x_bytes[:].bitcast(I32))
         nc.vector.tensor_copy(
-            staged[:, 0:S].rearrange("p (t m) -> p t m", t=PACK),
+            staged[:, S : 2 * S].rearrange("p (t m) -> p t m", t=PACK),
             d_bytes[:].rearrange("p (m t) -> p t m", t=PACK),
         )
         for q in range(4):
             nc.scalar.dma_start(
-                planes[32 * q : 32 * q + 4, :].bitcast(I32),
+                moved[32 * q : 32 * q + 4, :].bitcast(I32),
                 staged[32 * q : 32 * q + 32 : 8, :].bitcast(I32),
             )
-
-        w_raw = keep.tile([P, PACK, S], F32, name="w_raw", tag="early")
+        w_raw = keep.tile([P, PACK, S], F32, name="w_raw", tag="staged")
         nc.sync.dma_start(w_raw[:], w1.rearrange("(p t) m -> p t m", t=PACK))
+
         gain16 = keep.tile([P, PACK], F32, name="gain16")
-        inv_raw = keep.tile([P, PACK], F32, name="inv_raw")
-        inv_gain = keep.tile([P, PACK], F32, name="inv_gain")
-        d_picked = keep.tile([P, S], U32, name="d_picked", tag="d_gathered")
+        nc.gpsimd.tensor_scalar(gain16[:], gain[:], 0.0625, 0.0, ALU.mult, ALU.add)
+
+        d_picked = keep.tile([P, S], U32, name="d_picked", tag="d_bytes")
         d_codes = keep.tile([P, S], U32, name="d_codes", align_bytes=64)
         x_codes = keep.tile([P, S], U32, name="x_codes", align_bytes=64)
         nc.vector.tensor_copy(d_picked[:], d_table[:].indirect(lists["k1"][:]))
-        nc.vector.reciprocal(inv_raw[:], gain[:])
         nc.vector.tensor_copy(
             d_codes[:].rearrange("p (t m i) -> p m t i", t=PACK, i=PACK),
             d_picked[:].rearrange("p (m i t) -> p m t i", t=PACK, i=PACK),
         )
-        nc.gpsimd.tensor_scalar(gain16[:], gain[:], 0.0625, 0.0, ALU.mult, ALU.add)
-        nc.gpsimd.tensor_scalar(inv_gain[:], inv_raw[:], BIG, -BIG, ALU.min, ALU.max)
-        nc.vector.tensor_copy(x_codes[:], x_table[:].indirect(lists["offs"][:]))
+        nc.vector.tensor_copy(x_codes[:, 0:HALF], x_table[:].indirect(entries("offs", 0, HALF)))
+        nc.vector.tensor_copy(x_codes[:, HALF:S], x_table[:].indirect(entries("offs", HALF, HALF)))
+        inv_raw = keep.tile([P, PACK], F32, name="inv_raw", tag="x_table")
+        inv_gain = keep.tile([P, PACK], F32, name="inv_gain")
+        nc.vector.reciprocal(inv_raw[:], gain[:])
+        nc.vector.tensor_scalar(inv_gain[:], inv_raw[:], BIG, -BIG, ALU.min, ALU.max)
 
         gh = [keep.tile([P, S], F32, name="gh%d" % t) for t in range(PACK)]
         gate = [keep.tile([P, PACK, HALF], F32, name="gate%d" % half) for half in range(2)]
         far = [keep.tile([P, PACK, HALF], F32, name="far%d" % half) for half in range(2)]
         near = [keep.tile([P, PACK, HALF], F32, name="near%d" % half) for half in range(2)]
-        fetched = keep.tile([P, PACK, HALF], F32, name="fetched")
-        def first_product(t, bank, a, n):
+        fetched = [keep.tile([P, PACK, HALF], F32, name="fetched%d" % half) for half in range(2)]
+
+        def first_product(t, a, n, tag, engine):
+            bank = psum.tile([P, n], F32, name="h%d_%d" % (t, a), tag=tag)
             nc.tensor.matmul_mx(
                 out=bank[:],
                 lhsT=d_codes[:, t * P : (t + 1) * P].bitcast(FP8X4),
-                lhsT_scale=planes[:, t * P : (t + 1) * P],
+                lhsT_scale=moved[:, S + t * P : S + (t + 1) * P],
                 rhs=x_codes[:, a : a + n].bitcast(FP8X4),
-                rhs_scale=planes[:, S + a : S + a + n],
+                rhs_scale=moved[:, a : a + n],
                 start=True,
                 stop=True,
             )
-
-        def empty_h(t):
-            if t < 2:
-                for half in range(2):
-                    bank = psum.tile([P, HALF], F32, name="h%d%d" % (t, half), tag="bank%d" % (2 * t + half))
-                    first_product(t, bank, half * HALF, HALF)
-                    nc.vector.tensor_scalar(gh[t][:, cols(half)], bank[:], gain16[:, t : t + 1], None, ALU.mult)
+            if engine == "vector":
+                nc.vector.tensor_scalar(gh[t][:, a : a + n], bank[:], gain16[:, t : t + 1], None, ALU.mult)
             else:
-                bank = psum.tile([P, S], F32, name="h%d" % t, tag="bank%d" % (2 * (t - 2) + 1))
-                first_product(t, bank, 0, S)
-                nc.scalar.activation(gh[t][:], bank[:], ACT.Copy, scale=gain16[:, t : t + 1])
+                nc.scalar.activation(gh[t][:, a : a + n], bank[:], ACT.Copy, scale=gain16[:, t : t + 1])
 
         shared = [(2, 1), (3, 1)]
 
         def gate_of(t, half):
-            nc.scalar.activation(gate[half][:, t, :], gh[t][:].indirect(entries(lists["n1"], half)), ACT.Sigmoid, scale=inv_gain[:, t : t + 1])
-
-        def fetch(t, half):
-            nc.scalar.activation(fetched[:, t, :], gh[t][:].indirect(entries(lists["n2"], half)), ACT.Copy)
+            nc.scalar.activation(gate[half][:, t, :], gh[t][:].indirect(entries("n1", half * HALF, HALF)), ACT.Sigmoid, scale=inv_gain[:, t : t + 1])
+            if (t, half) in shared:
+                nc.scalar.activation(fetched[half][:, t, :], gh[t][:].indirect(entries("n2", half * HALF, HALF)), ACT.Copy)
 
         def blend(t, half):
+            own = gh[t][:, half * HALF : (half + 1) * HALF]
             if (t, half) in shared:
-                nc.vector.tensor_tensor(far[half][:, t, :], fetched[:, t, :], gate[half][:, t, :], ALU.mult)
+                nc.vector.scalar_tensor_tensor(near[half][:, t, :], gate[half][:, t, :], 1.0, own, ALU.subtract, ALU.mult)
+                nc.vector.tensor_tensor(far[half][:, t, :], fetched[half][:, t, :], gate[half][:, t, :], ALU.mult)
             else:
-                nc.vector.tensor_tensor(far[half][:, t, :], gh[t][:].indirect(entries(lists["n2"], half)), gate[half][:, t, :], ALU.mult)
-            nc.vector.scalar_tensor_tensor(near[half][:, t, :], gate[half][:, t, :], 1.0, gh[t][:, cols(half)], ALU.subtract, ALU.mult)
+                nc.vector.tensor_tensor(far[half][:, t, :], gh[t][:].indirect(entries("n2", half * HALF, HALF)), gate[half][:, t, :], ALU.mult)
+                nc.vector.scalar_tensor_tensor(near[half][:, t, :], gate[half][:, t, :], 1.0, own, ALU.subtract, ALU.mult)
 
         pieces = [(0, 256), (256, 128), (384, 128)]
         z_bf = [keep.tile([P, PACK * n], BF16, name="z_bf%d" % k, align_bytes=64) for k, (a, n) in enumerate(pieces)]
@@ -164,31 +161,27 @@ def tile_picked_hpqtracklap_none_p_kernel(tc, x_words, x_scales, d_words, d_scal
         w_codes = [keep.tile([P, HALF], U32, name="w_codes%d" % half, align_bytes=64) for half in range(2)]
         w_scales = [keep.tile([P, HALF], U8, name="w_scales%d" % half, align_bytes=64) for half in range(2)]
 
-        def round_w(half):
+        def round_w(b):
             nc.scalar.copy(
-                w_bf[half][:].rearrange("p (c i t) -> p c t i", i=4, t=PACK),
-                w_raw[:, :, cols(half)].rearrange("p t (c i) -> p c t i", i=4),
+                w_bf[b // 2][:, (b % 2) * S : (b % 2 + 1) * S].rearrange("p (c i t) -> p c t i", i=4, t=PACK),
+                w_raw[:, :, b * P : (b + 1) * P].rearrange("p t (c i) -> p c t i", i=4),
             )
 
         def quantize_w(half):
             nc.vector.quantize_mx(out=w_codes[half][:].bitcast(FP8X4), scales=w_scales[half][:], in_=w_bf[half][:])
 
-        banks2 = {}
-        scaled = [keep.tile([P, S], F32, name="scaled%d" % b) for b in range(PACK)]
+        banks2 = [psum.tile([P, S], F32, name="h2_%d" % b, tag="bank%d" % (4 + b)) for b in range(PACK)]
         third = [keep.tile([P, S], F32, name="third%d" % b) for b in range(PACK)]
+        fourth = [keep.tile([P, S], F32, name="fourth%d" % b) for b in range(PACK)]
         both = [keep.tile([P, S], F32, name="both%d" % b) for b in range(PACK)]
         result = [keep.tile([P, S], F32, name="result%d" % b) for b in range(PACK)]
-        fourth = keep.tile([P, S], F32, name="fourth")
-        negated = keep.tile([P, HALF], F32, name="negated")
-        for b in range(PACK):
-            for half in range(2):
-                banks2[b, half] = psum.tile([P, HALF], F32, name="h2_%d%d" % (b, half), tag="bank%d" % (2 * b + half))
+        negated = keep.tile([P, S], F32, name="negated")
 
         def second_product(k, b):
             a, n = pieces[k]
             within = slice((b % 2) * P, (b % 2 + 1) * P)
             nc.tensor.matmul_mx(
-                out=banks2[b, a // HALF][:, a % HALF : a % HALF + n],
+                out=banks2[b][:, a : a + n],
                 lhsT=w_codes[b // 2][:, within].bitcast(FP8X4),
                 lhsT_scale=w_scales[b // 2][:, within],
                 rhs=z_codes[k][:].bitcast(FP8X4),
@@ -197,52 +190,60 @@ def tile_picked_hpqtracklap_none_p_kernel(tc, x_words, x_scales, d_words, d_scal
                 stop=True,
             )
 
-        def empty_h2(b, half, engine):
+        def empty_h2(b, a, n, engine):
             if engine == "scalar":
-                nc.scalar.activation(scaled[b][:, cols(half)], banks2[b, half][:], ACT.Copy, scale=0.75)
+                nc.scalar.activation(scaled[b][:, a : a + n], banks2[b][:, a : a + n], ACT.Copy, scale=0.75)
             else:
-                nc.vector.tensor_scalar(scaled[b][:, cols(half)], banks2[b, half][:], 0.75, None, ALU.mult)
+                nc.vector.tensor_scalar(scaled[b][:, a : a + n], banks2[b][:, a : a + n], 0.75, None, ALU.mult)
 
-        def fetch3(b, half):
-            nc.scalar.activation(third[b][:, cols(half)], scaled[b][:].indirect(entries(lists["n3"], half)), ACT.Copy)
+        def negate(b, a, n):
+            nc.scalar.activation(negated[:, a : a + n], banks2[b][:, a : a + n], ACT.Copy, scale=-1.0)
 
-        def fetch4(b, half):
-            nc.scalar.activation(fourth[:, cols(half)], scaled[b][:].indirect(entries(lists["n4"], half)), ACT.Copy)
+        def fetch3(b, a, n):
+            nc.scalar.activation(third[b][:, a : a + n], scaled[b][:].indirect(entries("n3", a, n)), ACT.Copy)
 
-        def add4(b, half):
-            nc.vector.tensor_tensor(both[b][:, cols(half)], scaled[b][:].indirect(entries(lists["n4"], half)), third[b][:, cols(half)], ALU.add)
+        def fetch4(b, a, n):
+            nc.scalar.activation(fourth[b][:, a : a + n], scaled[b][:].indirect(entries("n4", a, n)), ACT.Copy)
 
-        def add_plain(b, half):
-            nc.vector.tensor_tensor(both[b][:, cols(half)], fourth[:, cols(half)], third[b][:, cols(half)], ALU.add)
+        def add4(b, a, n):
+            nc.vector.tensor_tensor(both[b][:, a : a + n], scaled[b][:].indirect(entries("n4", a, n)), third[b][:, a : a + n], ALU.add)
 
-        def less_h2(b, half):
-            nc.vector.tensor_tensor(result[b][:, cols(half)], both[b][:, cols(half)], banks2[b, half][:], ALU.subtract)
+        def add_plain(b, a, n):
+            nc.vector.tensor_tensor(both[b][:, a : a + n], fourth[b][:, a : a + n], third[b][:, a : a + n], ALU.add)
 
-        def store(b, half):
-            if half is None:
-                nc.sync.dma_start(out[b * P : (b + 1) * P, :], result[b][:])
-            else:
-                nc.sync.dma_start(out[b * P : (b + 1) * P, cols(half)], result[b][:, cols(half)])
+        def less_h2(b, a, n):
+            nc.vector.tensor_tensor(result[b][:, a : a + n], both[b][:, a : a + n], banks2[b][:, a : a + n], ALU.subtract)
 
-        empty_h(0)
+        def own4(b, a, n):
+            nc.vector.tensor_tensor(both[b][:, a : a + n], scaled[b][:].indirect(entries("n4", a, n)), negated[:, a : a + n], ALU.add)
+
+        def own3(b, a, n):
+            nc.vector.tensor_tensor(result[b][:, a : a + n], scaled[b][:].indirect(entries("n3", a, n)), both[b][:, a : a + n], ALU.add)
+
+        def store(b, a, n):
+            nc.sync.dma_start(out[b * P : (b + 1) * P, a : a + n], result[b][:, a : a + n])
+
+        first_product(0, 0, HALF, "bank0", "vector")
+        first_product(0, HALF, HALF, "bank1", "vector")
         gate_of(0, 0)
-        empty_h(1)
-        gate_of(1, 0)
+        first_product(1, 0, HALF, "bank0", "vector")
+        first_product(1, HALF, HALF, "bank2", "vector")
         gate_of(0, 1)
+        gate_of(1, 0)
         gate_of(1, 1)
-        empty_h(2)
+        first_product(2, 0, S, "bank1", "scalar")
         gate_of(2, 0)
-        empty_h(3)
+        first_product(3, 0, S, "bank2", "scalar")
         gate_of(3, 0)
         gate_of(2, 1)
         gate_of(3, 1)
-        for t, half in shared:
-            fetch(t, half)
         round_w(0)
         round_w(1)
+        round_w(2)
+        round_w(3)
         blend(0, 0)
-        blend(1, 0)
         blend(0, 1)
+        blend(1, 0)
         blend(1, 1)
         blend(2, 0)
         blend(3, 0)
@@ -258,43 +259,37 @@ def tile_picked_hpqtracklap_none_p_kernel(tc, x_words, x_scales, d_words, d_scal
         quantize_z(2)
         for b in range(PACK):
             second_product(0, b)
-        for b in range(PACK):
-            empty_h2(b, 0, "scalar")
-        nc.scalar.activation(negated[:], banks2[0, 0][:], ACT.Copy, scale=-1.0)
+        empty_h2(0, 0, HALF, "scalar")
+        negate(0, 0, HALF)
+        for b in range(1, PACK):
+            empty_h2(b, 0, HALF, "scalar")
         for b in range(PACK):
             second_product(1, b)
             second_product(2, b)
-        empty_h2(0, 1, "vector")
-        nc.vector.tensor_tensor(both[0][:, cols(0)], scaled[0][:].indirect(entries(lists["n4"], 0)), negated[:], ALU.add)
-        empty_h2(1, 1, "scalar")
-        fetch3(0, 1)
-        nc.vector.tensor_tensor(result[0][:, cols(0)], scaled[0][:].indirect(entries(lists["n3"], 0)), both[0][:, cols(0)], ALU.add)
-        add4(0, 1)
-        fetch3(1, 0)
-        fetch3(1, 1)
-        add4(1, 0)
-        less_h2(0, 1)
-        store(0, None)
-        empty_h2(2, 1, "scalar")
-        fetch3(2, 0)
-        fetch3(2, 1)
-        add4(1, 1)
-        less_h2(1, 0)
-        add4(2, 0)
-        less_h2(1, 1)
-        store(1, None)
-        empty_h2(3, 1, "scalar")
-        fetch3(3, 0)
-        fetch4(3, 0)
-        fetch3(3, 1)
-        fetch4(3, 1)
-        add4(2, 1)
-        less_h2(2, 0)
-        less_h2(2, 1)
-        store(2, None)
-        add_plain(3, 0)
-        less_h2(3, 0)
-        store(3, 0)
-        add_plain(3, 1)
-        less_h2(3, 1)
-        store(3, 1)
+        empty_h2(0, HALF, HALF, "vector")
+        empty_h2(1, HALF, HALF, "scalar")
+        own4(0, 0, HALF)
+        fetch3(0, HALF, HALF)
+        fetch3(1, 0, S)
+        empty_h2(2, HALF, HALF, "scalar")
+        fetch3(2, 0, S)
+        empty_h2(3, HALF, HALF, "scalar")
+        fetch3(3, 0, HALF)
+        fetch4(3, 0, HALF)
+        fetch3(3, HALF, HALF)
+        own3(0, 0, HALF)
+        add4(0, HALF, HALF)
+        add4(1, 0, S)
+        less_h2(0, HALF, HALF)
+        store(0, 0, S)
+        less_h2(1, 0, S)
+        store(1, 0, S)
+        add4(2, 0, S)
+        less_h2(2, 0, S)
+        store(2, 0, S)
+        add_plain(3, 0, HALF)
+        add4(3, HALF, HALF)
+        less_h2(3, 0, HALF)
+        store(3, 0, HALF)
+        less_h2(3, HALF, HALF)
+        store(3, HALF, HALF)

@@ -101,7 +101,7 @@ def tile_picked_hpqtracklap_none_p_kernel(tc, x_words, x_scales, d_words, d_scal
         nc.vector.tensor_scalar(inv_gain[:], inv_raw[:], BIG, -BIG, ALU.min, ALU.max)
 
         gh = [keep.tile([P, S], F32, name="gh%d" % t) for t in range(PACK)]
-        gate = [keep.tile([P, PACK, HALF], F32, name="gate%d" % half) for half in range(2)]
+        gate = [keep.tile([P, PACK, HALF], F32, name="gate%d" % half, tag="gate%d" % half, align_bytes=64) for half in range(2)]
         far = [keep.tile([P, PACK, HALF], F32, name="far%d" % half) for half in range(2)]
         near = [keep.tile([P, PACK, HALF], F32, name="near%d" % half) for half in range(2)]
         fetched = [keep.tile([P, PACK, HALF], F32, name="fetched%d" % half) for half in range(2)]
@@ -157,20 +157,27 @@ def tile_picked_hpqtracklap_none_p_kernel(tc, x_words, x_scales, d_words, d_scal
         def quantize_z(k):
             nc.vector.quantize_mx(out=z_codes[k][:].bitcast(FP8X4), scales=z_scales[k][:], in_=z_bf[k][:])
 
-        w_bf = [keep.tile([P, PACK * HALF], BF16, name="w_bf%d" % half, align_bytes=64) for half in range(2)]
+        w_bf = []
         w_codes = [keep.tile([P, HALF], U32, name="w_codes%d" % half, align_bytes=64) for half in range(2)]
         w_scales = [keep.tile([P, HALF], U8, name="w_scales%d" % half, align_bytes=64) for half in range(2)]
 
-        def round_w(b):
+        def round_w(half):
             nc.scalar.copy(
-                w_bf[b // 2][:, (b % 2) * S : (b % 2 + 1) * S].rearrange("p (c i t) -> p c t i", i=4, t=PACK),
-                w_raw[:, :, b * P : (b + 1) * P].rearrange("p t (c i) -> p c t i", i=4),
+                w_bf[0][:, half, :].rearrange("p (c i t) -> p c t i", i=4, t=PACK),
+                w_raw[:, :, half * HALF : (half + 1) * HALF].rearrange("p t (c i) -> p c t i", i=4),
             )
 
         def quantize_w(half):
-            nc.vector.quantize_mx(out=w_codes[half][:].bitcast(FP8X4), scales=w_scales[half][:], in_=w_bf[half][:])
+            nc.vector.quantize_mx(out=w_codes[half][:].bitcast(FP8X4), scales=w_scales[half][:], in_=w_bf[0][:, half, :])
 
         banks2 = [psum.tile([P, S], F32, name="h2_%d" % b, tag="bank%d" % (4 + b)) for b in range(PACK)]
+        first_half = psum.tile([P, HALF], F32, name="h2_first", tag="bank3")
+
+        def h2(b, a, n):
+            if b == 0 and a < HALF:
+                return first_half[:, a : a + n]
+            return banks2[b][:, a : a + n]
+
         third = [keep.tile([P, S], F32, name="third%d" % b) for b in range(PACK)]
         fourth = [keep.tile([P, S], F32, name="fourth%d" % b) for b in range(PACK)]
         both = [keep.tile([P, S], F32, name="both%d" % b) for b in range(PACK)]
@@ -181,7 +188,7 @@ def tile_picked_hpqtracklap_none_p_kernel(tc, x_words, x_scales, d_words, d_scal
             a, n = pieces[k]
             within = slice((b % 2) * P, (b % 2 + 1) * P)
             nc.tensor.matmul_mx(
-                out=banks2[b][:, a : a + n],
+                out=h2(b, a, n),
                 lhsT=w_codes[b // 2][:, within].bitcast(FP8X4),
                 lhsT_scale=w_scales[b // 2][:, within],
                 rhs=z_codes[k][:].bitcast(FP8X4),
@@ -192,12 +199,12 @@ def tile_picked_hpqtracklap_none_p_kernel(tc, x_words, x_scales, d_words, d_scal
 
         def empty_h2(b, a, n, engine):
             if engine == "scalar":
-                nc.scalar.activation(scaled[b][:, a : a + n], banks2[b][:, a : a + n], ACT.Copy, scale=0.75)
+                nc.scalar.activation(scaled[b][:, a : a + n], h2(b, a, n), ACT.Copy, scale=0.75)
             else:
-                nc.vector.tensor_scalar(scaled[b][:, a : a + n], banks2[b][:, a : a + n], 0.75, None, ALU.mult)
+                nc.vector.tensor_scalar(scaled[b][:, a : a + n], h2(b, a, n), 0.75, None, ALU.mult)
 
         def negate(b, a, n):
-            nc.scalar.activation(negated[:, a : a + n], banks2[b][:, a : a + n], ACT.Copy, scale=-1.0)
+            nc.scalar.activation(negated[:, a : a + n], h2(b, a, n), ACT.Copy, scale=-1.0)
 
         def fetch3(b, a, n):
             nc.scalar.activation(third[b][:, a : a + n], scaled[b][:].indirect(entries("n3", a, n)), ACT.Copy)
@@ -212,7 +219,7 @@ def tile_picked_hpqtracklap_none_p_kernel(tc, x_words, x_scales, d_words, d_scal
             nc.vector.tensor_tensor(both[b][:, a : a + n], fourth[b][:, a : a + n], third[b][:, a : a + n], ALU.add)
 
         def less_h2(b, a, n):
-            nc.vector.tensor_tensor(result[b][:, a : a + n], both[b][:, a : a + n], banks2[b][:, a : a + n], ALU.subtract)
+            nc.vector.tensor_tensor(result[b][:, a : a + n], both[b][:, a : a + n], h2(b, a, n), ALU.subtract)
 
         def own4(b, a, n):
             nc.vector.tensor_tensor(both[b][:, a : a + n], scaled[b][:].indirect(entries("n4", a, n)), negated[:, a : a + n], ALU.add)
@@ -223,7 +230,7 @@ def tile_picked_hpqtracklap_none_p_kernel(tc, x_words, x_scales, d_words, d_scal
         def store(b, a, n):
             nc.sync.dma_start(out[b * P : (b + 1) * P, a : a + n], result[b][:, a : a + n])
 
-        first_product(0, 0, HALF, "bank0", "vector")
+        first_product(0, 0, HALF, "bank0", "scalar")
         first_product(0, HALF, HALF, "bank1", "vector")
         gate_of(0, 0)
         first_product(1, 0, HALF, "bank0", "vector")
@@ -237,23 +244,22 @@ def tile_picked_hpqtracklap_none_p_kernel(tc, x_words, x_scales, d_words, d_scal
         gate_of(3, 0)
         gate_of(2, 1)
         gate_of(3, 1)
-        round_w(0)
-        round_w(1)
-        round_w(2)
-        round_w(3)
         blend(0, 0)
         blend(0, 1)
         blend(1, 0)
         blend(1, 1)
         blend(2, 0)
         blend(3, 0)
-        round_z(0)
+        w_bf.append(keep.tile([P, 2, PACK * HALF], BF16, name="w_bf", tag="gate0", align_bytes=64))
+        round_w(0)
+        round_w(1)
         blend(2, 1)
+        round_z(0)
+        blend(3, 1)
         quantize_z(0)
         quantize_w(0)
-        blend(3, 1)
-        quantize_w(1)
         round_z(1)
+        quantize_w(1)
         round_z(2)
         quantize_z(1)
         quantize_z(2)
@@ -277,17 +283,17 @@ def tile_picked_hpqtracklap_none_p_kernel(tc, x_words, x_scales, d_words, d_scal
         fetch3(3, 0, HALF)
         fetch4(3, 0, HALF)
         fetch3(3, HALF, HALF)
-        own3(0, 0, HALF)
         add4(0, HALF, HALF)
+        own3(0, 0, HALF)
         add4(1, 0, S)
         less_h2(0, HALF, HALF)
         store(0, 0, S)
         less_h2(1, 0, S)
         store(1, 0, S)
         add4(2, 0, S)
+        add_plain(3, 0, HALF)
         less_h2(2, 0, S)
         store(2, 0, S)
-        add_plain(3, 0, HALF)
         add4(3, HALF, HALF)
         less_h2(3, 0, HALF)
         store(3, 0, HALF)

@@ -283,6 +283,7 @@ def tile_picked_hpqtracklap_none_p_kernel(tc, x_words, x_scales, d_words, d_scal
         fetch3(3, 0, HALF)
         fetch4(3, 0, HALF)
         fetch3(3, HALF, HALF)
+        fetch4(3, HALF, HALF)
         add4(0, HALF, HALF)
         own3(0, 0, HALF)
         add4(1, 0, S)
@@ -294,8 +295,8 @@ def tile_picked_hpqtracklap_none_p_kernel(tc, x_words, x_scales, d_words, d_scal
         add_plain(3, 0, HALF)
         less_h2(2, 0, S)
         store(2, 0, S)
-        add4(3, HALF, HALF)
         less_h2(3, 0, HALF)
         store(3, 0, HALF)
+        add_plain(3, HALF, HALF)
         less_h2(3, HALF, HALF)
         store(3, HALF, HALF)

from contextlib import ExitStack

import concourse.mybir as mybir

F32 = mybir.dt.float32
BF16 = mybir.dt.bfloat16
I32 = mybir.dt.int32
U32 = mybir.dt.uint32
U16 = mybir.dt.uint16
U8 = mybir.dt.uint8
FP8X4 = mybir.dt.float8_e4m3fn_x4
ALU = mybir.AluOpType
ACT = mybir.ActivationFunctionType

P = 128
PACK = 4
T = 2048
S = 512
HALF = 256
SPARE = 16
FLOPS = 2 * 2 * 512 * 512 * 512
BIG = 3.0e38


def tile_picked_hpqtracklap_none_p_kernel(tc, x_words, x_scales, d_words, d_scales, gn, w1, offs, k1, n1, n2, n3, n4, out):
    nc = tc.nc
    with ExitStack() as ctx:
        keep = ctx.enter_context(tc.tile_pool(name="keep", bufs=1))
        psum = ctx.enter_context(tc.psum_pool(name="psum", bufs=1))

        def entries(name, a, n):
            return lists[name][:, a // 16 : (a + n) // 16]

        x_rows = keep.tile([P, T], U8, name="x_rows")
        d_rows = keep.tile([P, T], U8, name="d_rows")
        moved = keep.tile([P, 2 * S], U8, name="moved", align_bytes=64)
        scaled = [keep.tile([P, S + SPARE], F32, name="scaled%d" % b) for b in range(PACK)]
        nc.vector.memset(x_rows[:].bitcast(I32), 0)
        nc.vector.memset(d_rows[:].bitcast(I32), 0)
        warm_in = keep.tile([P, 1], F32, name="warm_in")
        warm_out = keep.tile([P, 1], F32, name="warm_out")
        nc.vector.memset(warm_in[:], 0.0)
        nc.scalar.activation(warm_out[:], warm_in[:], ACT.Sigmoid)
        nc.vector.memset(moved[:].bitcast(I32), 0)
        for b in range(PACK):
            nc.vector.memset(scaled[b][:, S : S + SPARE], 0.0)

        lists = {}
        for name in ("offs", "k1", "n1", "n2", "n3", "n4"):
            lists[name] = keep.tile([P, S // 16], U16, name="list_" + name)
        gain = keep.tile([P, PACK], F32, name="gain")
        d_table = keep.tile([P, T], U32, name="d_table", tag="d_table")
        x_table = keep.tile([P, T], U32, name="x_table", tag="x_table")

        nc.sync.dma_start(lists["offs"][:], offs)
        nc.sync.dma_start(lists["k1"][:], k1)
        nc.sync.dma_start(x_rows[0:P:8, :].bitcast(I32), x_scales[0].bitcast(I32))
        nc.sync.dma_start(d_rows[0:P:8, :].bitcast(I32), d_scales[0].bitcast(I32))
        nc.sync.dma_start(gain[:], gn.rearrange("(p t) o -> p (t o)", t=PACK))
        nc.sync.dma_start(lists["n1"][:], n1)
        nc.sync.dma_start(lists["n2"][:], n2)
        nc.sync.dma_start(d_table[:].bitcast(I32), d_words[0].rearrange("p n t -> p (n t)").bitcast(I32))
        nc.sync.dma_start(x_table[:].bitcast(I32), x_words[0].rearrange("p n t -> p (n t)").bitcast(I32))
        nc.sync.dma_start(lists["n3"][:], n3)
        nc.sync.dma_start(lists["n4"][:], n4)

        x_bytes = keep.tile([P, S], U8, name="x_bytes")
        d_bytes = keep.tile([P, S], U8, name="d_bytes", tag="d_bytes")
        staged = keep.tile([P, 2 * S], U8, name="staged", tag="staged")
        nc.vector.tensor_copy(x_bytes[:], x_rows[:].indirect(lists["offs"][:]))
        nc.vector.tensor_copy(d_bytes[:], d_rows[:].indirect(lists["k1"][:]))
        nc.vector.tensor_copy(staged[:, 0:S].bitcast(I32), x_bytes[:].bitcast(I32))
        nc.vector.tensor_copy(
            staged[:, S : 2 * S].rearrange("p (t m) -> p t m", t=PACK),
            d_bytes[:].rearrange("p (m t) -> p t m", t=PACK),
        )
        for q in range(4):
            nc.scalar.dma_start(
                moved[32 * q : 32 * q + 4, :].bitcast(I32),
                staged[32 * q : 32 * q + 32 : 8, :].bitcast(I32),
            )
        w_raw = keep.tile([P, PACK, S], F32, name="w_raw", tag="staged")
        nc.sync.dma_start(w_raw[:], w1.rearrange("(p t) m -> p t m", t=PACK))

        gain16 = keep.tile([P, PACK], F32, name="gain16")
        nc.gpsimd.tensor_scalar(gain16[:], gain[:], 0.0625, 0.0, ALU.mult, ALU.add)

        d_picked = keep.tile([P, S], U32, name="d_picked", tag="d_bytes")
        d_codes = keep.tile([P, S], U32, name="d_codes", align_bytes=64)
        x_codes = keep.tile([P, S], U32, name="x_codes", align_bytes=64)
        nc.vector.tensor_copy(d_picked[:], d_table[:].indirect(lists["k1"][:]))
        nc.vector.tensor_copy(
            d_codes[:].rearrange("p (t m i) -> p m t i", t=PACK, i=PACK),
            d_picked[:].rearrange("p (m i t) -> p m t i", t=PACK, i=PACK),
        )
        nc.vector.tensor_copy(x_codes[:, 0:HALF], x_table[:].indirect(entries("offs", 0, HALF)))
        nc.vector.tensor_copy(x_codes[:, HALF:S], x_table[:].indirect(entries("offs", HALF, HALF)))
        inv_raw = keep.tile([P, PACK], F32, name="inv_raw", tag="x_table")
        inv_gain = keep.tile([P, PACK], F32, name="inv_gain")
        nc.vector.reciprocal(inv_raw[:], gain[:])
        nc.vector.tensor_scalar(inv_gain[:], inv_raw[:], BIG, -BIG, ALU.min, ALU.max)

        gh = [keep.tile([P, S], F32, name="gh%d" % t) for t in range(PACK)]
        gate = [keep.tile([P, PACK, HALF], F32, name="gate%d" % half, tag="gate%d" % half, align_bytes=64) for half in range(2)]
        far = [keep.tile([P, PACK, HALF], F32, name="far%d" % half) for half in range(2)]
        near = [keep.tile([P, PACK, HALF], F32, name="near%d" % half) for half in range(2)]
        fetched = [keep.tile([P, PACK, HALF], F32, name="fetched%d" % half) for half in range(2)]

        def first_product(t, a, n, tag, engine):
            bank = psum.tile([P, n], F32, name="h%d_%d" % (t, a), tag=tag)
            nc.tensor.matmul_mx(
                out=bank[:],
                lhsT=d_codes[:, t * P : (t + 1) * P].bitcast(FP8X4),
                lhsT_scale=moved[:, S + t * P : S + (t + 1) * P],
                rhs=x_codes[:, a : a + n].bitcast(FP8X4),
                rhs_scale=moved[:, a : a + n],
                start=True,
                stop=True,
            )
            if engine == "vector":
                nc.vector.tensor_scalar(gh[t][:, a : a + n], bank[:], gain16[:, t : t + 1], None, ALU.mult)
            else:
                nc.scalar.activation(gh[t][:, a : a + n], bank[:], ACT.Copy, scale=gain16[:, t : t + 1])

        shared = [(2, 1), (3, 1)]

        def gate_of(t, half):
            nc.scalar.activation(gate[half][:, t, :], gh[t][:].indirect(entries("n1", half * HALF, HALF)), ACT.Sigmoid, scale=inv_gain[:, t : t + 1])
            if (t, half) in shared:
                nc.scalar.activation(fetched[half][:, t, :], gh[t][:].indirect(entries("n2", half * HALF, HALF)), ACT.Copy)

        def blend(t, half):
            own = gh[t][:, half * HALF : (half + 1) * HALF]
            if (t, half) in shared:
                nc.vector.scalar_tensor_tensor(near[half][:, t, :], gate[half][:, t, :], 1.0, own, ALU.subtract, ALU.mult)
                nc.vector.tensor_tensor(far[half][:, t, :], fetched[half][:, t, :], gate[half][:, t, :], ALU.mult)
            else:
                nc.vector.tensor_tensor(far[half][:, t, :], gh[t][:].indirect(entries("n2", half * HALF, HALF)), gate[half][:, t, :], ALU.mult)
                nc.vector.scalar_tensor_tensor(near[half][:, t, :], gate[half][:, t, :], 1.0, own, ALU.subtract, ALU.mult)

        pieces = [(0, 256), (256, 128), (384, 128)]
        z_bf = [keep.tile([P, PACK * n], BF16, name="z_bf%d" % k, align_bytes=64) for k, (a, n) in enumerate(pieces)]
        z_codes = [keep.tile([P, n], U32, name="z_codes%d" % k, align_bytes=64) for k, (a, n) in enumerate(pieces)]
        z_scales = [keep.tile([P, n], U8, name="z_scales%d" % k, align_bytes=64) for k, (a, n) in enumerate(pieces)]

        def round_z(k):
            a, n = pieces[k]
            half = a // HALF
            within = slice(a % HALF, a % HALF + n)
            nc.vector.tensor_tensor(
                z_bf[k][:].rearrange("p (c i t) -> p c t i", i=2, t=PACK),
                far[half][:, :, within].rearrange("p t (c i) -> p c t i", i=2),
                near[half][:, :, within].rearrange("p t (c i) -> p c t i", i=2),
                ALU.subtract,
            )

        def quantize_z(k):
            nc.vector.quantize_mx(out=z_codes[k][:].bitcast(FP8X4), scales=z_scales[k][:], in_=z_bf[k][:])

        w_bf = []
        w_codes = [keep.tile([P, HALF], U32, name="w_codes%d" % half, align_bytes=64) for half in range(2)]
        w_scales = [keep.tile([P, HALF], U8, name="w_scales%d" % half, align_bytes=64) for half in range(2)]

        def round_w(half):
            nc.scalar.copy(
                w_bf[0][:, half, :].rearrange("p (c i t) -> p c t i", i=4, t=PACK),
                w_raw[:, :, half * HALF : (half + 1) * HALF].rearrange("p t (c i) -> p c t i", i=4),
            )

        def quantize_w(half):
            nc.vector.quantize_mx(out=w_codes[half][:].bitcast(FP8X4), scales=w_scales[half][:], in_=w_bf[0][:, half, :])

        banks2 = [psum.tile([P, S], F32, name="h2_%d" % b, tag="bank%d" % (4 + b)) for b in range(PACK)]
        first_half = psum.tile([P, HALF], F32, name="h2_first", tag="bank3")

        def h2(b, a, n):
            if b == 0 and a < HALF:
                return first_half[:, a : a + n]
            return banks2[b][:, a : a + n]

        third = [keep.tile([P, S], F32, name="third%d" % b) for b in range(PACK)]
        fourth = [keep.tile([P, S], F32, name="fourth%d" % b) for b in range(PACK)]
        both = [keep.tile([P, S], F32, name="both%d" % b) for b in range(PACK)]
        result = [keep.tile([P, S], F32, name="result%d" % b) for b in range(PACK)]
        negated = keep.tile([P, S], F32, name="negated")

        def second_product(k, b):
            a, n = pieces[k]
            within = slice((b % 2) * P, (b % 2 + 1) * P)
            nc.tensor.matmul_mx(
                out=h2(b, a, n),
                lhsT=w_codes[b // 2][:, within].bitcast(FP8X4),
                lhsT_scale=w_scales[b // 2][:, within],
                rhs=z_codes[k][:].bitcast(FP8X4),
                rhs_scale=z_scales[k][:],
                start=True,
                stop=True,
            )

        def empty_h2(b, a, n, engine):
            if engine == "scalar":
                nc.scalar.activation(scaled[b][:, a : a + n], h2(b, a, n), ACT.Copy, scale=0.75)
            else:
                nc.vector.tensor_scalar(scaled[b][:, a : a + n], h2(b, a, n), 0.75, None, ALU.mult)

        def negate(b, a, n):
            nc.scalar.activation(negated[:, a : a + n], h2(b, a, n), ACT.Copy, scale=-1.0)

        def fetch3(b, a, n):
            nc.scalar.activation(third[b][:, a : a + n], scaled[b][:].indirect(entries("n3", a, n)), ACT.Copy)

        def fetch4(b, a, n):
            nc.scalar.activation(fourth[b][:, a : a + n], scaled[b][:].indirect(entries("n4", a, n)), ACT.Copy)

        def add4(b, a, n):
            nc.vector.tensor_tensor(both[b][:, a : a + n], scaled[b][:].indirect(entries("n4", a, n)), third[b][:, a : a + n], ALU.add)

        def add_plain(b, a, n):
            nc.vector.tensor_tensor(both[b][:, a : a + n], fourth[b][:, a : a + n], third[b][:, a : a + n], ALU.add)

        def less_h2(b, a, n):
            nc.vector.tensor_tensor(result[b][:, a : a + n], both[b][:, a : a + n], h2(b, a, n), ALU.subtract)

        def own4(b, a, n):
            nc.vector.tensor_tensor(both[b][:, a : a + n], scaled[b][:].indirect(entries("n4", a, n)), negated[:, a : a + n], ALU.add)

        def own3(b, a, n):
            nc.vector.tensor_tensor(result[b][:, a : a + n], scaled[b][:].indirect(entries("n3", a, n)), both[b][:, a : a + n], ALU.add)

        def store(b, a, n):
            nc.sync.dma_start(out[b * P : (b + 1) * P, a : a + n], result[b][:, a : a + n])

        first_product(0, 0, HALF, "bank0", "scalar")
        first_product(0, HALF, HALF, "bank1", "vector")
        gate_of(0, 0)
        first_product(1, 0, HALF, "bank0", "vector")
        first_product(1, HALF, HALF, "bank2", "vector")
        gate_of(0, 1)
        gate_of(1, 0)
        gate_of(1, 1)
        first_product(2, 0, S, "bank1", "scalar")
        gate_of(2, 0)
        first_product(3, 0, S, "bank2", "scalar")
        gate_of(3, 0)
        gate_of(2, 1)
        gate_of(3, 1)
        blend(0, 0)
        blend(0, 1)
        blend(1, 0)
        blend(1, 1)
        blend(2, 0)
        blend(3, 0)
        w_bf.append(keep.tile([P, 2, PACK * HALF], BF16, name="w_bf", tag="gate0", align_bytes=64))
        round_w(0)
        round_w(1)
        blend(2, 1)
        round_z(0)
        blend(3, 1)
        quantize_z(0)
        quantize_w(0)
        round_z(1)
        quantize_w(1)
        round_z(2)
        quantize_z(1)
        quantize_z(2)
        for b in range(PACK):
            second_product(0, b)
        empty_h2(0, 0, HALF, "scalar")
        negate(0, 0, HALF)
        for b in range(1, PACK):
            empty_h2(b, 0, HALF, "scalar")
        for b in range(PACK):
            second_product(1, b)
            second_product(2, b)
        empty_h2(0, HALF, HALF, "vector")
        empty_h2(1, HALF, HALF, "scalar")
        own4(0, 0, HALF)
        fetch3(0, HALF, HALF)
        fetch3(1, 0, S)
        empty_h2(2, HALF, HALF, "scalar")
        fetch3(2, 0, S)
        empty_h2(3, HALF, HALF, "scalar")
        fetch3(3, 0, HALF)
        fetch4(3, 0, HALF)
        fetch3(3, HALF, HALF)
        fetch4(3, HALF, HALF)
        add4(0, HALF, HALF)
        own3(0, 0, HALF)
        add4(1, 0, S)
        less_h2(0, HALF, HALF)
        store(0, 0, S)
        less_h2(1, 0, S)
        store(1, 0, S)
        add4(2, 0, S)
        add_plain(3, 0, HALF)
        less_h2(2, 0, S)
        store(2, 0, S)
        less_h2(3, 0, HALF)
        store(3, 0, HALF)
        add_plain(3, HALF, HALF)
        less_h2(3, HALF, HALF)
        store(3, HALF, HALF)
